import numpy as np, ml_dtypes
CORES = [7,39,87,119,135,167,215,247,263,295,343,375,391,423,471,503]
N = 16
CB = 128
def setup_inputs(rng):
    return {"x": rng.standard_normal((N, 128, N * CB), dtype=np.float32).astype(ml_dtypes.bfloat16)}
def setup_inputs_big(rng):
    d = setup_inputs(rng)
    for k in ("x",): d[k] = (d[k].astype(np.float32) * 1024.0).astype(d[k].dtype)
    return d
def setup_inputs_small(rng):
    d = setup_inputs(rng)
    for k in ("x",): d[k] = (d[k].astype(np.float32) * (1 / 1024.0)).astype(d[k].dtype)
    return d
def setup_inputs_apart(rng):
    d = setup_inputs(rng)
    f = (10.0 ** rng.permutation(np.linspace(-1.5, 1.5, N))).astype(np.float32).reshape(N, 1, 1)
    for k in ("x",): d[k] = (d[k].astype(np.float32) * f).astype(d[k].dtype)
    return d
def reference(x):
    X = x.astype(np.float64)
    G = sum(X[j].T @ X[j] for j in range(N))
    y = np.full((N, CB, N * CB), np.nan)
    for r in range(N):
        y[r][:, :CB * r] = G[CB * r:CB * r + CB, :CB * r]
    return {"y": y.astype(ml_dtypes.bfloat16 if x.dtype != np.float64 else np.float64)}

@@ -1,0 +1,220 @@
+from concourse.bass import DstId, RemoteDMATransfer
+from concourse.mybir import AluOpType
+
+N = 16
+CB = 128
+W = N * CB
+CH = 512
+NQ = W // CH
+NBANK = 8
+NSLOT = 4
+MAXG = 10
+USE_HELPERS = True
+
+SCRATCH = {
+    "xg": ("sbuf", [128, NSLOT * W], "bfloat16"),
+    "so": ("sbuf", [128, W], "bfloat16"),
+    "sd": ("sbuf", [128, W], "bfloat16"),
+    "sr": ("sbuf", [128, W], "bfloat16"),
+    "lo": ("sbuf", [128, W], "bfloat16"),
+    "lc": ("sbuf", [128, W], "bfloat16"),
+    "ls": ("sbuf", [128, W], "bfloat16"),
+    "t1": ("sbuf", [128, W], "float32"),
+    "ob": ("sbuf", [128, W], "bfloat16"),
+    "hb": ("sbuf", [128, CH], "bfloat16"),
+}
+for _i in range(NBANK):
+    SCRATCH["ps%d" % _i] = ("psum", [128, CH], "float32")
+
+SEMAPHORES = (["ld", "hin", "snt", "st"]
+              + ["ar%d" % q for q in range(NQ)] + ["co%d" % q for q in range(NQ)] + ["cd%d" % q for q in range(NQ)]
+              + ["sf%d" % q for q in range(NQ)] + ["fin%d" % q for q in range(NQ)]
+              + ["pe%d" % k for k in range(MAXG)] + ["ev%d" % k for k in range(MAXG)])
+
+
+def _bits(mask):
+    return [i for i in range(32) if (mask >> i) & 1]
+
+
+def _count(mask):
+    return len(_bits(mask))
+
+
+def _helpers(T, topo, core):
+    ncores = (max(topo.host(c) for c in T.cores) + 1) * topo.CORES_PER_HOST
+    mates = [c for c in range(ncores) if c != core and topo.host(c) == topo.host(core) and topo.chip(c) == topo.chip(core)]
+    far = [c for c in mates if topo.die(c) != topo.die(core)]
+    near = [c for c in mates if topo.die(c) == topo.die(core)]
+    out = []
+    for i in range(NQ // 2):
+        out += [far[i], near[i]]
+    return out
+
+
+def _host_group(T, topo, core):
+    return [b for b in range(N) if topo.host(T.cores[b]) == topo.host(core)]
+
+
+def _send_quarter(g, T, topo, sender, rank, q, src):
+    grp = _host_group(T, topo, T.cores[rank])
+    base = grp.index(rank) * W + q * CH
+    peers = [T.cores[b] for b in grp if b != rank]
+    mask = topo.mask(sender, peers[0])
+    ids = []
+    for d in peers:
+        rid, pid = topo.addr(d, sender)
+        ids.append(DstId(rid=rid, pnc=pid))
+    g.remote_dma_fused([RemoteDMATransfer(dst_ids=ids, dma_engine_mask=mask, remote_sem=T.sem["ar%d" % q], srcs=[src],
+                                          dsts=[T.xg[:, base:base + CH] for _ in peers], alu_op=0)], local_sem=T.sem.snt)
+    return _count(mask)
+
+
+def _helper_program(g, core, T, topo):
+    for rank in range(N):
+        rc = T.cores[rank]
+        if topo.host(rc) == topo.host(core) and topo.chip(rc) == topo.chip(core):
+            hs = _helpers(T, topo, rc)
+            if core in hs:
+                q = hs.index(core)
+                g.wait_ge(T.sem.hin, _count(topo.mask(rc, core)) // NQ)
+                n = _send_quarter(g, T, topo, core, rank, q, T.hb[:, :])
+                g.wait_ge(T.sem.snt, n)
+
+
+def rank_program(g, core, T, topo):
+    rank = T.rank_of(core)
+    if rank is None:
+        if USE_HELPERS:
+            _helper_program(g, core, T, topo)
+        return
+    cores = T.cores
+    sem = T.sem
+    grp = _host_group(T, topo, core)
+    slot = grp.index(rank)
+    others = [s for s in range(len(grp)) if s != slot]
+
+    role = {}
+    for b in range(N):
+        if topo.chip(cores[b]) != topo.chip(core):
+            continue
+        if b == rank:
+            role[b] = "own"
+        elif not topo.may_write(core, cores[b]):
+            role[b] = "opp"
+        elif topo.same_plane(core, cores[b]):
+            role[b] = "rel"
+        else:
+            role[b] = "dir"
+    cable = [cores[b] for b in role if role[b] == "dir"][0]
+    neigh = [cores[b] for b in role if role[b] == "rel"][0]
+    order = ([b for b in role if role[b] == "opp"]
+             + sorted([b for b in role if role[b] in ("rel", "dir")], reverse=True)
+             + [rank])
+    groups = []
+    for b in order:
+        for q in reversed(range(NQ)):
+            lo, hi = q * CH, min(q * CH + CH, b * CB)
+            if hi > lo:
+                groups.append((role[b], b, q, lo, hi))
+    ng = len(groups)
+    bank = [T["ps%d" % (k % NBANK)] for k in range(ng)]
+
+    g.sync.dma_start(T.xg[:, slot * W:(slot + 1) * W], T.x[:, :]).then_inc(sem.ld, 16)
+
+    sent = 0
+    g.wait_ge(sem.ld, 16)
+    if USE_HELPERS:
+        hs = _helpers(T, topo, core)
+        trs = []
+        for q in range(NQ):
+            eng = _bits(topo.mask(core, hs[q]))
+            per = len(eng) // NQ
+            m = sum(1 << e for e in eng[q * per:(q + 1) * per])
+            rid, pid = topo.addr(hs[q], core)
+            trs.append(RemoteDMATransfer(dst_ids=[DstId(rid=rid, pnc=pid)], dma_engine_mask=m, remote_sem=sem.hin,
+                                         srcs=[T.xg[:, slot * W + q * CH:slot * W + (q + 1) * CH]], dsts=[T.hb[:, :]],
+                                         alu_op=0))
+            sent += per
+        g.remote_dma_fused(trs, local_sem=sem.snt)
+    else:
+        for q in reversed(range(NQ)):
+            sent += _send_quarter(g, T, topo, core, rank, q, T.xg[:, slot * W + q * CH:slot * W + (q + 1) * CH])
+
+    te = g.tensor
+
+    def mm(k, s, start, stop):
+        _, b, _, lo, hi = groups[k]
+        o = s * W
+        return te.matmul(bank[k][:, 0:hi - lo], T.xg[:, o + b * CB:o + (b + 1) * CB], T.xg[:, o + lo:o + hi],
+                         start=start, stop=stop)
+
+    te.wait_ge(sem.ld, 16)
+    npre = min(NBANK, ng)
+    for k in range(npre):
+        mm(k, slot, True, False)
+    seen = set()
+    arrive = len(others) * _count(topo.mask(core, neigh))
+    for k in range(ng):
+        _, b, q, lo, hi = groups[k]
+        for c in ((b * CB) // CH, q):
+            if c not in seen:
+                seen.add(c)
+                te.wait_ge(sem["ar%d" % c], arrive)
+        if k >= npre:
+            te.wait_ge(sem["ev%d" % (k - NBANK)], 1)
+            mm(k, slot, True, False)
+        for i, s in enumerate(others):
+            ins = mm(k, s, False, i == len(others) - 1)
+        ins.then_inc(sem["pe%d" % k], 1)
+    for c in range(NQ):
+        if c not in seen:
+            te.wait_ge(sem["ar%d" % c], arrive)
+
+    ve = g.vector
+    cmask = topo.mask(core, cable)
+    nmask = topo.mask(core, neigh)
+    sbuf_of = {"opp": T.so, "dir": T.sd, "rel": T.sr}
+    for k in range(ng):
+        r, b, q, lo, hi = groups[k]
+        ve.wait_ge(sem["pe%d" % k], 1)
+        if r != "own":
+            ve.tensor_copy(sbuf_of[r][:, lo:hi], bank[k][:, 0:hi - lo]).then_inc(sem["ev%d" % k], 1)
+        else:
+            ve.wait_ge(sem["cd%d" % q], _count(cmask))
+            ve.tensor_tensor(T.t1[:, lo:hi], bank[k][:, 0:hi - lo], T.lc[:, lo:hi], AluOpType.add).then_inc(sem["ev%d" % k], 1)
+            ve.wait_ge(sem["ev%d" % k], 1)
+            ve.wait_ge(sem["sf%d" % q], _count(nmask))
+            ve.tensor_tensor(T.ob[:, lo:hi], T.t1[:, lo:hi], T.ls[:, lo:hi], AluOpType.add).then_inc(sem["fin%d" % q], 1)
+
+    crid, cpid = topo.addr(cable, core)
+    nrid, npid = topo.addr(neigh, core)
+    for k in range(ng):
+        r, b, q, lo, hi = groups[k]
+        if r == "own":
+            continue
+        g.wait_ge(sem["ev%d" % k], 1)
+        if r == "opp":
+            g.remote_dma(out_ap=T.lo[:, lo:hi], in_ap=T.so[:, lo:hi], remote_sem=sem["co%d" % q], local_sem=sem.snt,
+                         pid=cpid, routing_id=crid, dma_engine_mask=cmask)
+            sent += _count(cmask)
+        elif r == "dir":
+            g.remote_dma(out_ap=T.lc[:, lo:hi], in_ap=T.sd[:, lo:hi], remote_sem=sem["cd%d" % q], local_sem=sem.snt,
+                         pid=cpid, routing_id=crid, dma_engine_mask=cmask)
+            sent += _count(cmask)
+        else:
+            g.wait_ge(sem["co%d" % q], _count(cmask))
+            g.remote_dma_fused([RemoteDMATransfer(dst_ids=[DstId(rid=nrid, pnc=npid)], dma_engine_mask=nmask,
+                                                  remote_sem=sem["sf%d" % q], srcs=[T.sr[:, lo:hi], T.lo[:, lo:hi]],
+                                                  dsts=[T.ls[:, lo:hi]], alu_op=1)], local_sem=sem.snt)
+            sent += _count(nmask)
+    g.wait_ge(sem.snt, sent)
+
+    nst = 0
+    for k in range(ng):
+        r, b, q, lo, hi = groups[k]
+        if r == "own":
+            g.sync.wait_ge(sem["fin%d" % q], 1)
+            g.sync.dma_start(T.y[:, lo:hi], T.ob[:, lo:hi]).then_inc(sem.st, 16)
+            nst += 16
+    if nst:
+        g.sync.wait_ge(sem.st, nst)

@@ -10,6 +10,7 @@ NBANK = 8
 NSLOT = 4
 MAXG = 10
 USE_HELPERS = True
+CABLE_FIRST = False
 
 SCRATCH = {
     "xg": ("sbuf", [128, NSLOT * W], "bfloat16"),
@@ -173,6 +174,10 @@ def rank_program(g, core, T, topo):
     ve = g.vector
     cmask = topo.mask(core, cable)
     nmask = topo.mask(core, neigh)
+    fold_role = "rel" if CABLE_FIRST else "dir"
+    adds = [(T.lc, "cd", _count(cmask)), (T.ls, "sf", _count(nmask))]
+    if not CABLE_FIRST:
+        adds.reverse()
     sbuf_of = {"opp": T.so, "dir": T.sd, "rel": T.sr}
     for k in range(ng):
         r, b, q, lo, hi = groups[k]
@@ -180,33 +185,33 @@ def rank_program(g, core, T, topo):
         if r != "own":
             ve.tensor_copy(sbuf_of[r][:, lo:hi], bank[k][:, 0:hi - lo]).then_inc(sem["ev%d" % k], 1)
         else:
-            ve.wait_ge(sem["cd%d" % q], _count(cmask))
-            ve.tensor_tensor(T.t1[:, lo:hi], bank[k][:, 0:hi - lo], T.lc[:, lo:hi], AluOpType.add).then_inc(sem["ev%d" % k], 1)
+            ve.wait_ge(sem["%s%d" % (adds[0][1], q)], adds[0][2])
+            ve.tensor_tensor(T.t1[:, lo:hi], bank[k][:, 0:hi - lo], adds[0][0][:, lo:hi], AluOpType.add).then_inc(sem["ev%d" % k], 1)
             ve.wait_ge(sem["ev%d" % k], 1)
-            ve.wait_ge(sem["sf%d" % q], _count(nmask))
-            ve.tensor_tensor(T.ob[:, lo:hi], T.t1[:, lo:hi], T.ls[:, lo:hi], AluOpType.add).then_inc(sem["fin%d" % q], 1)
+            ve.wait_ge(sem["%s%d" % (adds[1][1], q)], adds[1][2])
+            ve.tensor_tensor(T.ob[:, lo:hi], T.t1[:, lo:hi], adds[1][0][:, lo:hi], AluOpType.add).then_inc(sem["fin%d" % q], 1)
 
-    crid, cpid = topo.addr(cable, core)
-    nrid, npid = topo.addr(neigh, core)
+    via = cable if CABLE_FIRST else neigh
     for k in range(ng):
         r, b, q, lo, hi = groups[k]
         if r == "own":
             continue
         g.wait_ge(sem["ev%d" % k], 1)
         if r == "opp":
-            g.remote_dma(out_ap=T.lo[:, lo:hi], in_ap=T.so[:, lo:hi], remote_sem=sem["co%d" % q], local_sem=sem.snt,
-                         pid=cpid, routing_id=crid, dma_engine_mask=cmask)
-            sent += _count(cmask)
+            dst, land, rs, srcs = via, T.lo, "co", [T.so[:, lo:hi]]
         elif r == "dir":
-            g.remote_dma(out_ap=T.lc[:, lo:hi], in_ap=T.sd[:, lo:hi], remote_sem=sem["cd%d" % q], local_sem=sem.snt,
-                         pid=cpid, routing_id=crid, dma_engine_mask=cmask)
-            sent += _count(cmask)
+            dst, land, rs, srcs = cable, T.lc, "cd", [T.sd[:, lo:hi]]
         else:
-            g.wait_ge(sem["co%d" % q], _count(cmask))
-            g.remote_dma_fused([RemoteDMATransfer(dst_ids=[DstId(rid=nrid, pnc=npid)], dma_engine_mask=nmask,
-                                                  remote_sem=sem["sf%d" % q], srcs=[T.sr[:, lo:hi], T.lo[:, lo:hi]],
-                                                  dsts=[T.ls[:, lo:hi]], alu_op=1)], local_sem=sem.snt)
-            sent += _count(nmask)
+            dst, land, rs, srcs = neigh, T.ls, "sf", [T.sr[:, lo:hi]]
+        if r == fold_role:
+            g.wait_ge(sem["co%d" % q], _count(topo.mask(via, core)))
+            srcs.append(T.lo[:, lo:hi])
+        rid, pid = topo.addr(dst, core)
+        m = topo.mask(core, dst)
+        g.remote_dma_fused([RemoteDMATransfer(dst_ids=[DstId(rid=rid, pnc=pid)], dma_engine_mask=m, remote_sem=sem["%s%d" % (rs, q)],
+                                              srcs=srcs, dsts=[land[:, lo:hi]], alu_op=1 if len(srcs) > 1 else 0)],
+                           local_sem=sem.snt)
+        sent += _count(m)
     g.wait_ge(sem.snt, sent)
 
     nst = 0

@@ -9,8 +9,6 @@ NQ = W // CH
 NBANK = 8
 NSLOT = 4
 MAXG = 10
-USE_HELPERS = True
-CABLE_FIRST = False
 
 SCRATCH = {
     "xg": ("sbuf", [128, NSLOT * W], "bfloat16"),
@@ -27,7 +25,7 @@ SCRATCH = {
 for _i in range(NBANK):
     SCRATCH["ps%d" % _i] = ("psum", [128, CH], "float32")
 
-SEMAPHORES = (["ld", "hin", "snt", "st"]
+SEMAPHORES = (["ld", "hin", "hd", "snt", "st"]
               + ["ar%d" % q for q in range(NQ)] + ["co%d" % q for q in range(NQ)] + ["cd%d" % q for q in range(NQ)]
               + ["sf%d" % q for q in range(NQ)] + ["fin%d" % q for q in range(NQ)]
               + ["pe%d" % k for k in range(MAXG)] + ["ev%d" % k for k in range(MAXG)])
@@ -41,59 +39,39 @@ def _count(mask):
     return len(_bits(mask))
 
 
+def _pair(topo, c):
+    return (c % topo.CORES_PER_CHIP) // 2
+
+
 def _helpers(T, topo, core):
     ncores = (max(topo.host(c) for c in T.cores) + 1) * topo.CORES_PER_HOST
     mates = [c for c in range(ncores) if c != core and topo.host(c) == topo.host(core) and topo.chip(c) == topo.chip(core)]
-    far = [c for c in mates if topo.die(c) != topo.die(core)]
-    near = [c for c in mates if topo.die(c) == topo.die(core)]
+    lead, rest, pairs = [], [], {_pair(topo, core)}
+    for c in mates:
+        if _pair(topo, c) in pairs:
+            rest.append(c)
+        else:
+            pairs.add(_pair(topo, c))
+            lead.append(c)
+    far = [c for c in lead + rest if topo.die(c) != topo.die(core)]
+    near = [c for c in lead + rest if topo.die(c) == topo.die(core)]
     out = []
     for i in range(NQ // 2):
         out += [far[i], near[i]]
     return out
 
 
+def _agent(T, topo, core, q):
+    return core if q == 0 else _helpers(T, topo, core)[q - 1]
+
+
 def _host_group(T, topo, core):
     return [b for b in range(N) if topo.host(T.cores[b]) == topo.host(core)]
 
 
-def _send_quarter(g, T, topo, sender, rank, q, src):
-    grp = _host_group(T, topo, T.cores[rank])
-    base = grp.index(rank) * W + q * CH
-    peers = [T.cores[b] for b in grp if b != rank]
-    mask = topo.mask(sender, peers[0])
-    ids = []
-    for d in peers:
-        rid, pid = topo.addr(d, sender)
-        ids.append(DstId(rid=rid, pnc=pid))
-    g.remote_dma_fused([RemoteDMATransfer(dst_ids=ids, dma_engine_mask=mask, remote_sem=T.sem["ar%d" % q], srcs=[src],
-                                          dsts=[T.xg[:, base:base + CH] for _ in peers], alu_op=0)], local_sem=T.sem.snt)
-    return _count(mask)
-
-
-def _helper_program(g, core, T, topo):
-    for rank in range(N):
-        rc = T.cores[rank]
-        if topo.host(rc) == topo.host(core) and topo.chip(rc) == topo.chip(core):
-            hs = _helpers(T, topo, rc)
-            if core in hs:
-                q = hs.index(core)
-                g.wait_ge(T.sem.hin, _count(topo.mask(rc, core)) // NQ)
-                n = _send_quarter(g, T, topo, core, rank, q, T.hb[:, :])
-                g.wait_ge(T.sem.snt, n)
-
-
-def rank_program(g, core, T, topo):
-    rank = T.rank_of(core)
-    if rank is None:
-        if USE_HELPERS:
-            _helper_program(g, core, T, topo)
-        return
+def _plan(T, topo, rank):
     cores = T.cores
-    sem = T.sem
-    grp = _host_group(T, topo, core)
-    slot = grp.index(rank)
-    others = [s for s in range(len(grp)) if s != slot]
-
+    core = cores[rank]
     role = {}
     for b in range(N):
         if topo.chip(cores[b]) != topo.chip(core):
@@ -117,6 +95,65 @@ def rank_program(g, core, T, topo):
             lo, hi = q * CH, min(q * CH + CH, b * CB)
             if hi > lo:
                 groups.append((role[b], b, q, lo, hi))
+    return cable, neigh, groups
+
+
+def _write(g, T, topo, src_core, dst, srcs, out, rsem, mask=None):
+    rid, pid = topo.addr(dst, src_core)
+    m = topo.mask(src_core, dst) if mask is None else mask
+    g.remote_dma_fused([RemoteDMATransfer(dst_ids=[DstId(rid=rid, pnc=pid)], dma_engine_mask=m, remote_sem=rsem, srcs=srcs,
+                                          dsts=[out], alu_op=1 if len(srcs) > 1 else 0)], local_sem=T.sem.snt)
+    return _count(m)
+
+
+def _send_quarter(g, T, topo, sender, rank, q, src):
+    grp = _host_group(T, topo, T.cores[rank])
+    base = grp.index(rank) * W + q * CH
+    peers = [T.cores[b] for b in grp if b != rank]
+    mask = topo.mask(sender, peers[0])
+    ids = []
+    for d in peers:
+        rid, pid = topo.addr(d, sender)
+        ids.append(DstId(rid=rid, pnc=pid))
+    g.remote_dma_fused([RemoteDMATransfer(dst_ids=ids, dma_engine_mask=mask, remote_sem=T.sem["ar%d" % q], srcs=[src],
+                                          dsts=[T.xg[:, base:base + CH] for _ in peers], alu_op=0)], local_sem=T.sem.snt)
+    return _count(mask)
+
+
+def _chip_mask(topo, core, helper, off):
+    return topo.mask(core, helper) & ~topo.mask(core, off)
+
+
+def _helper_program(g, core, T, topo):
+    for rank in range(N):
+        rc = T.cores[rank]
+        if topo.host(rc) != topo.host(core) or topo.chip(rc) != topo.chip(core):
+            continue
+        hs = _helpers(T, topo, rc)
+        if core not in hs:
+            continue
+        q = hs.index(core)
+        g.wait_ge(T.sem.hin, _count(topo.mask(rc, core)) // NQ)
+        n = _send_quarter(g, T, topo, core, rank, q, T.hb[:, :])
+        cable, neigh, groups = _plan(T, topo, rank)
+        for r, b, p, lo, hi in groups:
+            if r == "dir" and _agent(T, topo, rc, p) == core:
+                g.wait_ge(T.sem["co%d" % p], _count(topo.mask(neigh, core)))
+                g.wait_ge(T.sem.hd, _count(_chip_mask(topo, rc, core, neigh)))
+                n += _write(g, T, topo, core, cable, [T.sd[:, lo:hi], T.lo[:, lo:hi]], T.lc[:, lo:hi], T.sem["cd%d" % p])
+        g.wait_ge(T.sem.snt, n)
+
+
+def rank_program(g, core, T, topo):
+    rank = T.rank_of(core)
+    if rank is None:
+        _helper_program(g, core, T, topo)
+        return
+    sem = T.sem
+    grp = _host_group(T, topo, core)
+    slot = grp.index(rank)
+    others = [s for s in range(len(grp)) if s != slot]
+    cable, neigh, groups = _plan(T, topo, rank)
     ng = len(groups)
     bank = [T["ps%d" % (k % NBANK)] for k in range(ng)]
 
@@ -124,22 +161,18 @@ def rank_program(g, core, T, topo):
 
     sent = 0
     g.wait_ge(sem.ld, 16)
-    if USE_HELPERS:
-        hs = _helpers(T, topo, core)
-        trs = []
-        for q in range(NQ):
-            eng = _bits(topo.mask(core, hs[q]))
-            per = len(eng) // NQ
-            m = sum(1 << e for e in eng[q * per:(q + 1) * per])
-            rid, pid = topo.addr(hs[q], core)
-            trs.append(RemoteDMATransfer(dst_ids=[DstId(rid=rid, pnc=pid)], dma_engine_mask=m, remote_sem=sem.hin,
-                                         srcs=[T.xg[:, slot * W + q * CH:slot * W + (q + 1) * CH]], dsts=[T.hb[:, :]],
-                                         alu_op=0))
-            sent += per
-        g.remote_dma_fused(trs, local_sem=sem.snt)
-    else:
-        for q in reversed(range(NQ)):
-            sent += _send_quarter(g, T, topo, core, rank, q, T.xg[:, slot * W + q * CH:slot * W + (q + 1) * CH])
+    hs = _helpers(T, topo, core)
+    trs = []
+    for q in range(NQ):
+        eng = _bits(topo.mask(core, hs[q]))
+        per = len(eng) // NQ
+        m = sum(1 << e for e in eng[q * per:(q + 1) * per])
+        rid, pid = topo.addr(hs[q], core)
+        trs.append(RemoteDMATransfer(dst_ids=[DstId(rid=rid, pnc=pid)], dma_engine_mask=m, remote_sem=sem.hin,
+                                     srcs=[T.xg[:, slot * W + q * CH:slot * W + (q + 1) * CH]], dsts=[T.hb[:, :]],
+                                     alu_op=0))
+        sent += per
+    g.remote_dma_fused(trs, local_sem=sem.snt)
 
     te = g.tensor
 
@@ -172,12 +205,8 @@ def rank_program(g, core, T, topo):
             te.wait_ge(sem["ar%d" % c], arrive)
 
     ve = g.vector
-    cmask = topo.mask(core, cable)
-    nmask = topo.mask(core, neigh)
-    fold_role = "rel" if CABLE_FIRST else "dir"
-    adds = [(T.lc, "cd", _count(cmask)), (T.ls, "sf", _count(nmask))]
-    if not CABLE_FIRST:
-        adds.reverse()
+    ncab = _count(topo.mask(cable, core))
+    nsw = _count(topo.mask(neigh, core))
     sbuf_of = {"opp": T.so, "dir": T.sd, "rel": T.sr}
     for k in range(ng):
         r, b, q, lo, hi = groups[k]
@@ -185,33 +214,29 @@ def rank_program(g, core, T, topo):
         if r != "own":
             ve.tensor_copy(sbuf_of[r][:, lo:hi], bank[k][:, 0:hi - lo]).then_inc(sem["ev%d" % k], 1)
         else:
-            ve.wait_ge(sem["%s%d" % (adds[0][1], q)], adds[0][2])
-            ve.tensor_tensor(T.t1[:, lo:hi], bank[k][:, 0:hi - lo], adds[0][0][:, lo:hi], AluOpType.add).then_inc(sem["ev%d" % k], 1)
+            ve.wait_ge(sem["sf%d" % q], nsw)
+            ve.tensor_tensor(T.t1[:, lo:hi], bank[k][:, 0:hi - lo], T.ls[:, lo:hi], AluOpType.add).then_inc(sem["ev%d" % k], 1)
             ve.wait_ge(sem["ev%d" % k], 1)
-            ve.wait_ge(sem["%s%d" % (adds[1][1], q)], adds[1][2])
-            ve.tensor_tensor(T.ob[:, lo:hi], T.t1[:, lo:hi], adds[1][0][:, lo:hi], AluOpType.add).then_inc(sem["fin%d" % q], 1)
+            ve.wait_ge(sem["cd%d" % q], ncab)
+            ve.tensor_tensor(T.ob[:, lo:hi], T.t1[:, lo:hi], T.lc[:, lo:hi], AluOpType.add).then_inc(sem["fin%d" % q], 1)
 
-    via = cable if CABLE_FIRST else neigh
     for k in range(ng):
         r, b, q, lo, hi = groups[k]
         if r == "own":
             continue
         g.wait_ge(sem["ev%d" % k], 1)
         if r == "opp":
-            dst, land, rs, srcs = via, T.lo, "co", [T.so[:, lo:hi]]
-        elif r == "dir":
-            dst, land, rs, srcs = cable, T.lc, "cd", [T.sd[:, lo:hi]]
+            sent += _write(g, T, topo, core, _agent(T, topo, neigh, q), [T.so[:, lo:hi]], T.lo[:, lo:hi], sem["co%d" % q])
+        elif r == "rel":
+            sent += _write(g, T, topo, core, neigh, [T.sr[:, lo:hi]], T.ls[:, lo:hi], sem["sf%d" % q])
         else:
-            dst, land, rs, srcs = neigh, T.ls, "sf", [T.sr[:, lo:hi]]
-        if r == fold_role:
-            g.wait_ge(sem["co%d" % q], _count(topo.mask(via, core)))
-            srcs.append(T.lo[:, lo:hi])
-        rid, pid = topo.addr(dst, core)
-        m = topo.mask(core, dst)
-        g.remote_dma_fused([RemoteDMATransfer(dst_ids=[DstId(rid=rid, pnc=pid)], dma_engine_mask=m, remote_sem=sem["%s%d" % (rs, q)],
-                                              srcs=srcs, dsts=[land[:, lo:hi]], alu_op=1 if len(srcs) > 1 else 0)],
-                           local_sem=sem.snt)
-        sent += _count(m)
+            a = _agent(T, topo, core, q)
+            if a == core:
+                g.wait_ge(sem["co%d" % q], nsw)
+                sent += _write(g, T, topo, core, cable, [T.sd[:, lo:hi], T.lo[:, lo:hi]], T.lc[:, lo:hi], sem["cd%d" % q])
+            else:
+                sent += _write(g, T, topo, core, a, [T.sd[:, lo:hi]], T.sd[:, lo:hi], sem.hd,
+                               mask=_chip_mask(topo, core, a, neigh))
     g.wait_ge(sem.snt, sent)
 
     nst = 0

@@ -6,29 +6,35 @@ CB = 128
 W = N * CB
 CH = 512
 NQ = W // CH
-NBANK = 8
 NSLOT = 4
-MAXG = 10
+PK = (NQ - 1) * CB
+ORDER = ("opp", "dir", "rel", "own")
 
 SCRATCH = {
-    "xg": ("sbuf", [128, NSLOT * W], "bfloat16"),
-    "so": ("sbuf", [128, W], "bfloat16"),
-    "sd": ("sbuf", [128, W], "bfloat16"),
-    "sr": ("sbuf", [128, W], "bfloat16"),
-    "lo": ("sbuf", [128, W], "bfloat16"),
-    "lc": ("sbuf", [128, W], "bfloat16"),
+    "xs": ("sbuf", [128, W], "bfloat16"),
+    "xp": ("sbuf", [128, NSLOT * PK], "bfloat16"),
+    "pb": ("sbuf", [128, PK], "bfloat16"),
+    "xq": ("sbuf", [128, NSLOT * CH], "bfloat16"),
+    "lp": ("sbuf", [128, NSLOT * PK], "bfloat16"),
+    "so": ("sbuf", [128, CH], "bfloat16"),
+    "sd": ("sbuf", [128, CH], "bfloat16"),
+    "sr": ("sbuf", [128, CH], "bfloat16"),
+    "sw": ("sbuf", [128, CH], "bfloat16"),
+    "lo": ("sbuf", [128, CH], "bfloat16"),
+    "ow": ("sbuf", [128, W], "bfloat16"),
     "ls": ("sbuf", [128, W], "bfloat16"),
-    "t1": ("sbuf", [128, W], "float32"),
+    "lc": ("sbuf", [128, W], "bfloat16"),
     "ob": ("sbuf", [128, W], "bfloat16"),
-    "hb": ("sbuf", [128, CH], "bfloat16"),
 }
-for _i in range(NBANK):
+for _i in range(NQ):
     SCRATCH["ps%d" % _i] = ("psum", [128, CH], "float32")
 
-SEMAPHORES = (["ld", "hin", "hd", "snt", "st"]
-              + ["ar%d" % q for q in range(NQ)] + ["co%d" % q for q in range(NQ)] + ["cd%d" % q for q in range(NQ)]
-              + ["sf%d" % q for q in range(NQ)] + ["fin%d" % q for q in range(NQ)]
-              + ["pe%d" % k for k in range(MAXG)] + ["ev%d" % k for k in range(MAXG)])
+SEMAPHORES = (["ld", "pk", "hq", "hp", "ar", "co", "snt", "st"]
+              + ["ow%d" % q for q in range(NQ)] + ["sf%d" % q for q in range(NQ)] + ["cd%d" % q for q in range(NQ)]
+              + ["tq%d" % q for q in range(NQ)] + ["fin%d" % q for q in range(NQ)]
+              + ["pe%d" % k for k in range(NQ)] + ["ev%d" % k for k in range(NQ)])
+
+_MEMO = {}
 
 
 def _bits(mask):
@@ -39,212 +45,281 @@ def _count(mask):
     return len(_bits(mask))
 
 
-def _pair(topo, c):
-    return (c % topo.CORES_PER_CHIP) // 2
-
-
-def _helpers(T, topo, core):
-    ncores = (max(topo.host(c) for c in T.cores) + 1) * topo.CORES_PER_HOST
-    mates = [c for c in range(ncores) if c != core and topo.host(c) == topo.host(core) and topo.chip(c) == topo.chip(core)]
-    lead, rest, pairs = [], [], {_pair(topo, core)}
-    for c in mates:
-        if _pair(topo, c) in pairs:
-            rest.append(c)
-        else:
-            pairs.add(_pair(topo, c))
-            lead.append(c)
-    far = [c for c in lead + rest if topo.die(c) != topo.die(core)]
-    near = [c for c in lead + rest if topo.die(c) == topo.die(core)]
-    out = []
-    for i in range(NQ // 2):
-        out += [far[i], near[i]]
+def _one_a_die(topo, cs):
+    out, dies = [], set()
+    for c in cs:
+        if topo.die(c) not in dies:
+            dies.add(topo.die(c))
+            out.append(c)
     return out
 
 
-def _agent(T, topo, core, q):
-    return core if q == 0 else _helpers(T, topo, core)[q - 1]
+def _crew(T, topo, rc):
+    if rc not in _MEMO:
+        ncores = (max(topo.host(c) for c in T.cores) + 1) * topo.CORES_PER_HOST
+        here = [c for c in range(ncores) if c != rc and topo.host(c) == topo.host(rc) and topo.chip(c) == topo.chip(rc)]
+        there = [c for c in range(ncores) if topo.mates(c, rc)]
+        spares = [c for c in here if topo.may_write(c, there[0])][:NSLOT - 1]
+        load = lambda c: sum(1 for e in spares if topo.die(e) == topo.die(c))
+        near = sorted(_one_a_die(topo, [c for c in here if c not in spares]), key=load)
+        far = sorted(_one_a_die(topo, [c for c in there if topo.may_write(c, rc)]), key=load)
+        _MEMO[rc] = ([near[0], far[0], far[1], near[1]], spares)
+    return _MEMO[rc]
 
 
 def _host_group(T, topo, core):
     return [b for b in range(N) if topo.host(T.cores[b]) == topo.host(core)]
 
 
-def _plan(T, topo, rank):
-    cores = T.cores
-    core = cores[rank]
+def _roles(T, topo, rc):
     role = {}
     for b in range(N):
-        if topo.chip(cores[b]) != topo.chip(core):
+        c = T.cores[b]
+        if topo.chip(c) != topo.chip(rc):
             continue
-        if b == rank:
+        if c == rc:
             role[b] = "own"
-        elif not topo.may_write(core, cores[b]):
+        elif not topo.may_write(rc, c):
             role[b] = "opp"
-        elif topo.same_plane(core, cores[b]):
+        elif topo.same_plane(rc, c):
             role[b] = "rel"
         else:
             role[b] = "dir"
-    cable = [cores[b] for b in role if role[b] == "dir"][0]
-    neigh = [cores[b] for b in role if role[b] == "rel"][0]
-    order = ([b for b in role if role[b] == "opp"]
-             + sorted([b for b in role if role[b] in ("rel", "dir")], reverse=True)
-             + [rank])
-    groups = []
-    for b in order:
-        for q in reversed(range(NQ)):
+    return role
+
+
+def _pieces(T, topo, rc, q):
+    role = _roles(T, topo, rc)
+    out = []
+    for r in ORDER:
+        for b in role:
             lo, hi = q * CH, min(q * CH + CH, b * CB)
-            if hi > lo:
-                groups.append((role[b], b, q, lo, hi))
-    return cable, neigh, groups
+            if role[b] == r and hi > lo:
+                out.append((r, b, lo, hi))
+    return out
 
 
-def _write(g, T, topo, src_core, dst, srcs, out, rsem, mask=None):
-    rid, pid = topo.addr(dst, src_core)
-    m = topo.mask(src_core, dst) if mask is None else mask
-    g.remote_dma_fused([RemoteDMATransfer(dst_ids=[DstId(rid=rid, pnc=pid)], dma_engine_mask=m, remote_sem=rsem, srcs=srcs,
-                                          dsts=[out], alu_op=1 if len(srcs) > 1 else 0)], local_sem=T.sem.snt)
+def _packrows(T, topo, rc):
+    return [b for b in sorted(_roles(T, topo, rc), reverse=True) if (b * CB) // CH > 0]
+
+
+def _needs_pack(T, topo, rc, q):
+    return any((b * CB) // CH != q for _, b, _, _ in _pieces(T, topo, rc, q))
+
+
+def _pack_users(T, topo, rc):
+    return [_crew(T, topo, rc)[0][q] for q in range(NQ) if _needs_pack(T, topo, rc, q)]
+
+
+def _pack_classes(T, topo, rc):
+    need = {}
+    for q in range(NQ):
+        if _needs_pack(T, topo, rc, q):
+            need[_crew(T, topo, rc)[0][q]] = CB * sum(1 for b in _packrows(T, topo, rc) if (b * CB) // CH > q)
+    full = [c for c in need if need[c] == PK]
+    rest = [c for c in need if need[c] < PK]
+    out = [(PK, full)]
+    if rest:
+        out.append((max(need[c] for c in rest), rest))
+    return out
+
+
+def _per(T, topo, rc):
+    return _count(topo.mask(rc, _crew(T, topo, rc)[1][0])) // NQ
+
+
+def _deal(T, topo, rc, dests):
+    per = _per(T, topo, rc)
+    allowed = []
+    for ds in dests:
+        m = topo.mask(rc, ds[0])
+        for d in ds:
+            m &= topo.mask(rc, d)
+        allowed.append(m)
+    used, out = 0, {}
+    for i in sorted(range(len(dests)), key=lambda i: _count(allowed[i])):
+        m = sum(1 << e for e in _bits(allowed[i] & ~used)[:per])
+        used |= m
+        out[i] = m
+    return [out[i] for i in range(len(dests))]
+
+
+def _own_mask(topo, w, rc, off):
+    m = topo.mask(w, rc) & ~topo.mask(w, off)
+    return m if m else topo.mask(w, rc)
+
+
+def _transfer(topo, src_core, dsts, srcs, outs, rsem, mask):
+    ids = []
+    for d in dsts:
+        rid, pid = topo.addr(d, src_core)
+        ids.append(DstId(rid=rid, pnc=pid))
+    return RemoteDMATransfer(dst_ids=ids, dma_engine_mask=mask, remote_sem=rsem, srcs=srcs, dsts=outs,
+                             alu_op=1 if len(srcs) > 1 else 0)
+
+
+def _send(g, T, topo, src_core, dsts, srcs, out, rsem, mask=None):
+    m = topo.mask(src_core, dsts[0]) if mask is None else mask
+    g.remote_dma_fused([_transfer(topo, src_core, dsts, srcs, [out for _ in dsts], rsem, m)], local_sem=T.sem.snt)
     return _count(m)
 
 
-def _send_quarter(g, T, topo, sender, rank, q, src):
-    grp = _host_group(T, topo, T.cores[rank])
-    base = grp.index(rank) * W + q * CH
-    peers = [T.cores[b] for b in grp if b != rank]
-    mask = topo.mask(sender, peers[0])
-    ids = []
-    for d in peers:
-        rid, pid = topo.addr(d, sender)
-        ids.append(DstId(rid=rid, pnc=pid))
-    g.remote_dma_fused([RemoteDMATransfer(dst_ids=ids, dma_engine_mask=mask, remote_sem=T.sem["ar%d" % q], srcs=[src],
-                                          dsts=[T.xg[:, base:base + CH] for _ in peers], alu_op=0)], local_sem=T.sem.snt)
-    return _count(mask)
+def _spare_program(g, core, T, topo, rank, i):
+    rc = T.cores[rank]
+    grp = _host_group(T, topo, rc)
+    slot = grp.index(rank)
+    peer = T.cores[[b for b in grp if b != rank][i]]
+    g.wait_ge(T.sem.hq, _per(T, topo, rc))
+    n = 0
+    for wd, users in _pack_classes(T, topo, peer):
+        n += _send(g, T, topo, core, users, [T.pb[:, 0:wd]], T.lp[:, slot * PK:slot * PK + wd], T.sem.ar)
+    g.wait_ge(T.sem.snt, n)
 
 
-def _chip_mask(topo, core, helper, off):
-    return topo.mask(core, helper) & ~topo.mask(core, off)
+def _worker_program(g, core, T, topo, rank, q):
+    sem = T.sem
+    rc = T.cores[rank]
+    grp = _host_group(T, topo, rc)
+    slot = grp.index(rank)
+    others = [s for s in range(len(grp)) if s != slot]
+    role = _roles(T, topo, rc)
+    cable = [T.cores[b] for b in role if role[b] == "dir"][0]
+    neigh = [T.cores[b] for b in role if role[b] == "rel"][0]
+    twin = _crew(T, topo, neigh)[0][q]
+    pcs = _pieces(T, topo, rc, q)
+    pack = _needs_pack(T, topo, rc, q)
+    prow = _packrows(T, topo, rc)
+    nh = _per(T, topo, rc)
+    bank = [T["ps%d" % i] for i in range(len(pcs))]
+    mine = T.xq[:, slot * CH:(slot + 1) * CH]
 
+    sent = 0
+    g.wait_ge(sem.hq, nh)
+    peers = [_crew(T, topo, T.cores[b])[0][q] for b in grp if b != rank and _pieces(T, topo, T.cores[b], q)]
+    if peers:
+        sent += _send(g, T, topo, core, peers, [mine], mine, sem.ar)
 
-def _helper_program(g, core, T, topo):
-    for rank in range(N):
-        rc = T.cores[rank]
-        if topo.host(rc) != topo.host(core) or topo.chip(rc) != topo.chip(core):
-            continue
-        hs = _helpers(T, topo, rc)
-        if core not in hs:
-            continue
-        q = hs.index(core)
-        g.wait_ge(T.sem.hin, _count(topo.mask(rc, core)) // NQ)
-        n = _send_quarter(g, T, topo, core, rank, q, T.hb[:, :])
-        cable, neigh, groups = _plan(T, topo, rank)
-        for r, b, p, lo, hi in groups:
-            if r == "dir" and _agent(T, topo, rc, p) == core:
-                g.wait_ge(T.sem["co%d" % p], _count(topo.mask(neigh, core)))
-                g.wait_ge(T.sem.hd, _count(_chip_mask(topo, rc, core, neigh)))
-                n += _write(g, T, topo, core, cable, [T.sd[:, lo:hi], T.lo[:, lo:hi]], T.lc[:, lo:hi], T.sem["cd%d" % p])
-        g.wait_ge(T.sem.snt, n)
+    te = g.tensor
+
+    def mm(i, s, start, stop):
+        _, b, lo, hi = pcs[i]
+        if (b * CB) // CH == q:
+            o = s * CH + b * CB - q * CH
+            lhs = T.xq[:, o:o + CB]
+        else:
+            o = s * PK + prow.index(b) * CB
+            lhs = T.lp[:, o:o + CB]
+        return te.matmul(bank[i][:, 0:hi - lo], lhs, T.xq[:, s * CH:s * CH + hi - lo], start=start, stop=stop)
+
+    if pcs:
+        te.wait_ge(sem.hq, nh)
+        if pack:
+            te.wait_ge(sem.hp, nh)
+        for i in range(len(pcs)):
+            mm(i, slot, True, False)
+        te.wait_ge(sem.ar, len(others) * _count(topo.mask(twin, core)) * (2 if pack else 1))
+        for i in range(len(pcs)):
+            for j, s in enumerate(others):
+                ins = mm(i, s, False, j == len(others) - 1)
+            ins.then_inc(sem["pe%d" % i], 1)
+
+    stage = {"opp": T.so, "dir": T.sd, "rel": T.sr, "own": T.sw}
+    for i, (r, b, lo, hi) in enumerate(pcs):
+        g.vector.wait_ge(sem["pe%d" % i], 1)
+        g.vector.tensor_copy(stage[r][:, 0:hi - lo], bank[i][:, 0:hi - lo]).then_inc(sem["ev%d" % i], 1)
+
+    for i, (r, b, lo, hi) in enumerate(pcs):
+        w = hi - lo
+        g.wait_ge(sem["ev%d" % i], 1)
+        if r == "opp":
+            sent += _send(g, T, topo, core, [twin], [T.so[:, 0:w]], T.lo[:, 0:w], sem.co)
+        elif r == "dir":
+            g.wait_ge(sem.co, _count(topo.mask(twin, core)))
+            sent += _send(g, T, topo, core, [cable], [T.sd[:, 0:w], T.lo[:, 0:w]], T.lc[:, lo:hi], sem["cd%d" % q])
+        elif r == "rel":
+            sent += _send(g, T, topo, core, [neigh], [T.sr[:, 0:w]], T.ls[:, lo:hi], sem["sf%d" % q])
+        else:
+            sent += _send(g, T, topo, core, [rc], [T.sw[:, 0:w]], T.ow[:, lo:hi], sem["ow%d" % q],
+                          mask=_own_mask(topo, core, rc, neigh))
+    g.wait_ge(sem.snt, sent)
 
 
 def rank_program(g, core, T, topo):
     rank = T.rank_of(core)
     if rank is None:
-        _helper_program(g, core, T, topo)
+        for b in range(N):
+            rc = T.cores[b]
+            if topo.host(rc) == topo.host(core):
+                workers, spares = _crew(T, topo, rc)
+                if core in workers:
+                    _worker_program(g, core, T, topo, b, workers.index(core))
+                elif core in spares:
+                    _spare_program(g, core, T, topo, b, spares.index(core))
         return
     sem = T.sem
     grp = _host_group(T, topo, core)
     slot = grp.index(rank)
-    others = [s for s in range(len(grp)) if s != slot]
-    cable, neigh, groups = _plan(T, topo, rank)
-    ng = len(groups)
-    bank = [T["ps%d" % (k % NBANK)] for k in range(ng)]
+    workers, spares = _crew(T, topo, core)
+    role = _roles(T, topo, core)
+    cable = [T.cores[b] for b in role if role[b] == "dir"][0]
+    neigh = [T.cores[b] for b in role if role[b] == "rel"][0]
+    ve = g.vector
 
-    g.sync.dma_start(T.xg[:, slot * W:(slot + 1) * W], T.x[:, :]).then_inc(sem.ld, 16)
+    g.sync.dma_start(T.xs[:, :], T.x[:, :]).then_inc(sem.ld, 16)
+
+    ve.wait_ge(sem.ld, 16)
+    npk = 0
+    for d in [s for s in range(len(grp)) if s != slot] + [slot]:
+        for j, b in enumerate(_packrows(T, topo, T.cores[grp[d]])):
+            ve.tensor_copy(T.xp[:, d * PK + j * CB:d * PK + (j + 1) * CB], T.xs[:, b * CB:(b + 1) * CB]).then_inc(sem.pk, 1)
+            npk += 1
 
     sent = 0
     g.wait_ge(sem.ld, 16)
-    hs = _helpers(T, topo, core)
     trs = []
+    ms = _deal(T, topo, core, [[w] for w in workers])
     for q in range(NQ):
-        eng = _bits(topo.mask(core, hs[q]))
-        per = len(eng) // NQ
-        m = sum(1 << e for e in eng[q * per:(q + 1) * per])
-        rid, pid = topo.addr(hs[q], core)
-        trs.append(RemoteDMATransfer(dst_ids=[DstId(rid=rid, pnc=pid)], dma_engine_mask=m, remote_sem=sem.hin,
-                                     srcs=[T.xg[:, slot * W + q * CH:slot * W + (q + 1) * CH]], dsts=[T.hb[:, :]],
-                                     alu_op=0))
-        sent += per
+        trs.append(_transfer(topo, core, [workers[q]], [T.xs[:, q * CH:(q + 1) * CH]],
+                             [T.xq[:, slot * CH:(slot + 1) * CH]], sem.hq, ms[q]))
+        sent += _count(ms[q])
     g.remote_dma_fused(trs, local_sem=sem.snt)
-
-    te = g.tensor
-
-    def mm(k, s, start, stop):
-        _, b, _, lo, hi = groups[k]
-        o = s * W
-        return te.matmul(bank[k][:, 0:hi - lo], T.xg[:, o + b * CB:o + (b + 1) * CB], T.xg[:, o + lo:o + hi],
-                         start=start, stop=stop)
-
-    te.wait_ge(sem.ld, 16)
-    npre = min(NBANK, ng)
-    for k in range(npre):
-        mm(k, slot, True, False)
-    seen = set()
-    arrive = len(others) * _count(topo.mask(core, neigh))
-    for k in range(ng):
-        _, b, q, lo, hi = groups[k]
-        for c in ((b * CB) // CH, q):
-            if c not in seen:
-                seen.add(c)
-                te.wait_ge(sem["ar%d" % c], arrive)
-        if k >= npre:
-            te.wait_ge(sem["ev%d" % (k - NBANK)], 1)
-            mm(k, slot, True, False)
-        for i, s in enumerate(others):
-            ins = mm(k, s, False, i == len(others) - 1)
-        ins.then_inc(sem["pe%d" % k], 1)
-    for c in range(NQ):
-        if c not in seen:
-            te.wait_ge(sem["ar%d" % c], arrive)
-
-    ve = g.vector
-    ncab = _count(topo.mask(cable, core))
-    nsw = _count(topo.mask(neigh, core))
-    sbuf_of = {"opp": T.so, "dir": T.sd, "rel": T.sr}
-    for k in range(ng):
-        r, b, q, lo, hi = groups[k]
-        ve.wait_ge(sem["pe%d" % k], 1)
-        if r != "own":
-            ve.tensor_copy(sbuf_of[r][:, lo:hi], bank[k][:, 0:hi - lo]).then_inc(sem["ev%d" % k], 1)
-        else:
-            ve.wait_ge(sem["sf%d" % q], nsw)
-            ve.tensor_tensor(T.t1[:, lo:hi], bank[k][:, 0:hi - lo], T.ls[:, lo:hi], AluOpType.add).then_inc(sem["ev%d" % k], 1)
-            ve.wait_ge(sem["ev%d" % k], 1)
-            ve.wait_ge(sem["cd%d" % q], ncab)
-            ve.tensor_tensor(T.ob[:, lo:hi], T.t1[:, lo:hi], T.lc[:, lo:hi], AluOpType.add).then_inc(sem["fin%d" % q], 1)
-
-    for k in range(ng):
-        r, b, q, lo, hi = groups[k]
-        if r == "own":
-            continue
-        g.wait_ge(sem["ev%d" % k], 1)
-        if r == "opp":
-            sent += _write(g, T, topo, core, _agent(T, topo, neigh, q), [T.so[:, lo:hi]], T.lo[:, lo:hi], sem["co%d" % q])
-        elif r == "rel":
-            sent += _write(g, T, topo, core, neigh, [T.sr[:, lo:hi]], T.ls[:, lo:hi], sem["sf%d" % q])
-        else:
-            a = _agent(T, topo, core, q)
-            if a == core:
-                g.wait_ge(sem["co%d" % q], nsw)
-                sent += _write(g, T, topo, core, cable, [T.sd[:, lo:hi], T.lo[:, lo:hi]], T.lc[:, lo:hi], sem["cd%d" % q])
-            else:
-                sent += _write(g, T, topo, core, a, [T.sd[:, lo:hi]], T.sd[:, lo:hi], sem.hd,
-                               mask=_chip_mask(topo, core, a, neigh))
+    g.wait_ge(sem.pk, npk)
+    trs = []
+    users = _pack_users(T, topo, core)
+    ms = _deal(T, topo, core, [[e] for e in spares] + [users])
+    for i, d in enumerate([s for s in range(len(grp)) if s != slot]):
+        trs.append(_transfer(topo, core, [spares[i]], [T.xp[:, d * PK:(d + 1) * PK]], [T.pb[:, :]], sem.hq, ms[i]))
+        sent += _count(ms[i])
+    trs.append(_transfer(topo, core, users, [T.xp[:, slot * PK:(slot + 1) * PK]],
+                         [T.lp[:, slot * PK:(slot + 1) * PK] for _ in users], sem.hp, ms[-1]))
+    sent += _count(ms[-1])
+    g.remote_dma_fused(trs, local_sem=sem.snt)
     g.wait_ge(sem.snt, sent)
 
+    mine = [(q, q * CH, min(q * CH + CH, rank * CB)) for q in reversed(range(NQ)) if rank * CB > q * CH]
+
+    def first(q, lo, hi):
+        ve.wait_ge(sem["ow%d" % q], _count(_own_mask(topo, workers[q], core, neigh)))
+        ve.wait_ge(sem["sf%d" % q], _count(topo.mask(_crew(T, topo, neigh)[0][q], core)))
+        ve.tensor_tensor(T["ps%d" % q][:, 0:hi - lo], T.ow[:, lo:hi], T.ls[:, lo:hi], AluOpType.add).then_inc(sem["tq%d" % q], 1)
+
+    def last(q, lo, hi):
+        ve.wait_ge(sem["tq%d" % q], 1)
+        ve.wait_ge(sem["cd%d" % q], _count(topo.mask(_crew(T, topo, cable)[0][q], core)))
+        ve.tensor_tensor(T.ob[:, lo:hi], T["ps%d" % q][:, 0:hi - lo], T.lc[:, lo:hi], AluOpType.add).then_inc(sem["fin%d" % q], 1)
+
+    for p in mine[:-1]:
+        first(*p)
+    for p in mine[:-1]:
+        last(*p)
+    for p in mine[-1:]:
+        first(*p)
+        last(*p)
+
     nst = 0
-    for k in range(ng):
-        r, b, q, lo, hi = groups[k]
-        if r == "own":
-            g.sync.wait_ge(sem["fin%d" % q], 1)
-            g.sync.dma_start(T.y[:, lo:hi], T.ob[:, lo:hi]).then_inc(sem.st, 16)
-            nst += 16
+    for q, lo, hi in mine:
+        g.sync.wait_ge(sem["fin%d" % q], 1)
+        g.sync.dma_start(T.y[:, lo:hi], T.ob[:, lo:hi]).then_inc(sem.st, 16)
+        nst += 16
     if nst:
         g.sync.wait_ge(sem.st, nst)

@@ -8,7 +8,7 @@ CH = 512
 NQ = W // CH
 NSLOT = 4
 PK = (NQ - 1) * CB
-ORDER = ("opp", "dir", "rel", "own")
+ORDER = ("opp", "rel", "own", "dir")
 
 SCRATCH = {
     "xs": ("sbuf", [128, W], "bfloat16"),
@@ -29,7 +29,7 @@ SCRATCH = {
 for _i in range(NQ):
     SCRATCH["ps%d" % _i] = ("psum", [128, CH], "float32")
 
-SEMAPHORES = (["ld", "pk", "hq", "hp", "ar", "co", "snt", "st"]
+SEMAPHORES = (["ld", "pk", "hq", "hp", "co", "snt", "st0", "st1"] + ["a%d" % s for s in range(NSLOT)]
               + ["ow%d" % q for q in range(NQ)] + ["sf%d" % q for q in range(NQ)] + ["cd%d" % q for q in range(NQ)]
               + ["tq%d" % q for q in range(NQ)] + ["fin%d" % q for q in range(NQ)]
               + ["pe%d" % k for k in range(NQ)] + ["ev%d" % k for k in range(NQ)])
@@ -97,6 +97,15 @@ def _pieces(T, topo, rc, q):
             if role[b] == r and hi > lo:
                 out.append((r, b, lo, hi))
     return out
+
+
+def _reads(T, topo, rc, q):
+    u = 0
+    for _, b, lo, hi in _pieces(T, topo, rc, q):
+        u = max(u, hi - lo)
+        if (b * CB) // CH == q:
+            u = max(u, b * CB - q * CH + CB)
+    return u
 
 
 def _packrows(T, topo, rc):
@@ -172,7 +181,7 @@ def _spare_program(g, core, T, topo, rank, i):
     g.wait_ge(T.sem.hq, _per(T, topo, rc))
     n = 0
     for wd, users in _pack_classes(T, topo, peer):
-        n += _send(g, T, topo, core, users, [T.pb[:, 0:wd]], T.lp[:, slot * PK:slot * PK + wd], T.sem.ar)
+        n += _send(g, T, topo, core, users, [T.pb[:, 0:wd]], T.lp[:, slot * PK:slot * PK + wd], T.sem["a%d" % slot])
     g.wait_ge(T.sem.snt, n)
 
 
@@ -181,7 +190,7 @@ def _worker_program(g, core, T, topo, rank, q):
     rc = T.cores[rank]
     grp = _host_group(T, topo, rc)
     slot = grp.index(rank)
-    others = [s for s in range(len(grp)) if s != slot]
+    others = [(slot - d) % len(grp) for d in range(1, len(grp))]
     role = _roles(T, topo, rc)
     cable = [T.cores[b] for b in role if role[b] == "dir"][0]
     neigh = [T.cores[b] for b in role if role[b] == "rel"][0]
@@ -191,13 +200,15 @@ def _worker_program(g, core, T, topo, rank, q):
     prow = _packrows(T, topo, rc)
     nh = _per(T, topo, rc)
     bank = [T["ps%d" % i] for i in range(len(pcs))]
-    mine = T.xq[:, slot * CH:(slot + 1) * CH]
 
     sent = 0
     g.wait_ge(sem.hq, nh)
-    peers = [_crew(T, topo, T.cores[b])[0][q] for b in grp if b != rank and _pieces(T, topo, T.cores[b], q)]
-    if peers:
-        sent += _send(g, T, topo, core, peers, [mine], mine, sem.ar)
+    for d in range(1, len(grp)):
+        peer = T.cores[grp[(slot + d) % len(grp)]]
+        u = _reads(T, topo, peer, q)
+        if u:
+            part = T.xq[:, slot * CH:slot * CH + u]
+            sent += _send(g, T, topo, core, [_crew(T, topo, peer)[0][q]], [part], part, sem["a%d" % slot])
 
     te = g.tensor
 
@@ -211,16 +222,28 @@ def _worker_program(g, core, T, topo, rank, q):
             lhs = T.lp[:, o:o + CB]
         return te.matmul(bank[i][:, 0:hi - lo], lhs, T.xq[:, s * CH:s * CH + hi - lo], start=start, stop=stop)
 
+    def landed(s):
+        src = T.cores[grp[s]]
+        n = _count(topo.mask(_crew(T, topo, src)[0][q], core))
+        if pack:
+            n += _count(topo.mask(_crew(T, topo, src)[1][0], core))
+        te.wait_ge(sem["a%d" % s], n)
+
     if pcs:
         te.wait_ge(sem.hq, nh)
         if pack:
             te.wait_ge(sem.hp, nh)
         for i in range(len(pcs)):
             mm(i, slot, True, False)
-        te.wait_ge(sem.ar, len(others) * _count(topo.mask(twin, core)) * (2 if pack else 1))
+        landed(others[0])
         for i in range(len(pcs)):
-            for j, s in enumerate(others):
-                ins = mm(i, s, False, j == len(others) - 1)
+            mm(i, others[0], False, False)
+        late = others[1:]
+        for i in range(len(pcs)):
+            for s in late:
+                if i == 0:
+                    landed(s)
+                ins = mm(i, s, False, s == late[-1])
             ins.then_inc(sem["pe%d" % i], 1)
 
     stage = {"opp": T.so, "dir": T.sd, "rel": T.sr, "own": T.sw}
@@ -308,18 +331,18 @@ def rank_program(g, core, T, topo):
         ve.wait_ge(sem["cd%d" % q], _count(topo.mask(_crew(T, topo, cable)[0][q], core)))
         ve.tensor_tensor(T.ob[:, lo:hi], T["ps%d" % q][:, 0:hi - lo], T.lc[:, lo:hi], AluOpType.add).then_inc(sem["fin%d" % q], 1)
 
-    for p in mine[:-1]:
+    for p in mine:
         first(*p)
-    for p in mine[:-1]:
-        last(*p)
-    for p in mine[-1:]:
-        first(*p)
+    for p in mine:
         last(*p)
 
-    nst = 0
-    for q, lo, hi in mine:
-        g.sync.wait_ge(sem["fin%d" % q], 1)
-        g.sync.dma_start(T.y[:, lo:hi], T.ob[:, lo:hi]).then_inc(sem.st, 16)
-        nst += 16
-    if nst:
-        g.sync.wait_ge(sem.st, nst)
+    queues = [g.sync, g.scalar]
+    nst = [0, 0]
+    for k, (q, lo, hi) in enumerate(mine):
+        e = k % 2
+        queues[e].wait_ge(sem["fin%d" % q], 1)
+        queues[e].dma_start(T.y[:, lo:hi], T.ob[:, lo:hi]).then_inc(sem["st%d" % e], 16)
+        nst[e] += 16
+    for e in range(2):
+        if nst[e]:
+            queues[e].wait_ge(sem["st%d" % e], nst[e])

@@ -7,6 +7,7 @@ W = N * CB
 CH = 512
 NQ = W // CH
 NSLOT = 4
+NLD = 2
 PK = (NQ - 1) * CB
 ORDER = ("opp", "rel", "own", "dir")
 
@@ -29,7 +30,8 @@ SCRATCH = {
 for _i in range(NQ):
     SCRATCH["ps%d" % _i] = ("psum", [128, CH], "float32")
 
-SEMAPHORES = (["ld", "pk", "hq", "hp", "co", "snt", "st0", "st1"] + ["a%d" % s for s in range(NSLOT)]
+SEMAPHORES = (["ld%d" % k for k in range(NLD)] + ["pk", "hq", "hp", "co", "snt", "st0", "st1"]
+              + ["a%d" % s for s in range(NSLOT)]
               + ["ow%d" % q for q in range(NQ)] + ["sf%d" % q for q in range(NQ)] + ["cd%d" % q for q in range(NQ)]
               + ["tq%d" % q for q in range(NQ)] + ["fin%d" % q for q in range(NQ)]
               + ["pe%d" % k for k in range(NQ)] + ["ev%d" % k for k in range(NQ)])
@@ -125,20 +127,19 @@ def _pack_classes(T, topo, rc):
     for q in range(NQ):
         if _needs_pack(T, topo, rc, q):
             need[_crew(T, topo, rc)[0][q]] = CB * sum(1 for b in _packrows(T, topo, rc) if (b * CB) // CH > q)
-    full = [c for c in need if need[c] == PK]
-    rest = [c for c in need if need[c] < PK]
-    out = [(PK, full)]
-    if rest:
-        out.append((max(need[c] for c in rest), rest))
-    return out
+    return [(wd, [c for c in need if need[c] == wd]) for wd in sorted(set(need.values()), reverse=True)]
 
 
-def _per(T, topo, rc):
-    return _count(topo.mask(rc, _crew(T, topo, rc)[1][0])) // NQ
+def _served(grp, slot, i):
+    return (slot + 1 + i) % len(grp)
+
+
+def _per(T, topo, rc, n):
+    return _count(topo.mask(rc, _crew(T, topo, rc)[1][0])) // n
 
 
 def _deal(T, topo, rc, dests):
-    per = _per(T, topo, rc)
+    per = _per(T, topo, rc, len(dests))
     allowed = []
     for ds in dests:
         m = topo.mask(rc, ds[0])
@@ -177,8 +178,8 @@ def _spare_program(g, core, T, topo, rank, i):
     rc = T.cores[rank]
     grp = _host_group(T, topo, rc)
     slot = grp.index(rank)
-    peer = T.cores[[b for b in grp if b != rank][i]]
-    g.wait_ge(T.sem.hq, _per(T, topo, rc))
+    peer = T.cores[grp[_served(grp, slot, i)]]
+    g.wait_ge(T.sem.hq, _per(T, topo, rc, NSLOT))
     n = 0
     for wd, users in _pack_classes(T, topo, peer):
         n += _send(g, T, topo, core, users, [T.pb[:, 0:wd]], T.lp[:, slot * PK:slot * PK + wd], T.sem["a%d" % slot])
@@ -198,7 +199,8 @@ def _worker_program(g, core, T, topo, rank, q):
     pcs = _pieces(T, topo, rc, q)
     pack = _needs_pack(T, topo, rc, q)
     prow = _packrows(T, topo, rc)
-    nh = _per(T, topo, rc)
+    nh = _per(T, topo, rc, NQ // NLD)
+    nhp = _per(T, topo, rc, NSLOT)
     bank = [T["ps%d" % i] for i in range(len(pcs))]
 
     sent = 0
@@ -232,7 +234,7 @@ def _worker_program(g, core, T, topo, rank, q):
     if pcs:
         te.wait_ge(sem.hq, nh)
         if pack:
-            te.wait_ge(sem.hp, nh)
+            te.wait_ge(sem.hp, nhp)
         for i in range(len(pcs)):
             mm(i, slot, True, False)
         landed(others[0])
@@ -288,9 +290,13 @@ def rank_program(g, core, T, topo):
     neigh = [T.cores[b] for b in role if role[b] == "rel"][0]
     ve = g.vector
 
-    g.sync.dma_start(T.xs[:, :], T.x[:, :]).then_inc(sem.ld, 16)
+    LW = W // NLD
+    lq = [g.sync, g.scalar]
+    for k in range(NLD):
+        lq[k % 2].dma_start(T.xs[:, k * LW:(k + 1) * LW], T.x[:, k * LW:(k + 1) * LW]).then_inc(sem["ld%d" % k], 16)
 
-    ve.wait_ge(sem.ld, 16)
+    for k in range(NLD):
+        ve.wait_ge(sem["ld%d" % k], 16)
     npk = 0
     for d in [s for s in range(len(grp)) if s != slot] + [slot]:
         for j, b in enumerate(_packrows(T, topo, T.cores[grp[d]])):
@@ -298,19 +304,22 @@ def rank_program(g, core, T, topo):
             npk += 1
 
     sent = 0
-    g.wait_ge(sem.ld, 16)
-    trs = []
-    ms = _deal(T, topo, core, [[w] for w in workers])
-    for q in range(NQ):
-        trs.append(_transfer(topo, core, [workers[q]], [T.xs[:, q * CH:(q + 1) * CH]],
-                             [T.xq[:, slot * CH:(slot + 1) * CH]], sem.hq, ms[q]))
-        sent += _count(ms[q])
-    g.remote_dma_fused(trs, local_sem=sem.snt)
+    for k in range(NLD):
+        qs = list(range(k * NQ // NLD, (k + 1) * NQ // NLD))
+        g.wait_ge(sem["ld%d" % k], 16)
+        ms = _deal(T, topo, core, [[workers[q]] for q in qs])
+        trs = []
+        for i, q in enumerate(qs):
+            trs.append(_transfer(topo, core, [workers[q]], [T.xs[:, q * CH:(q + 1) * CH]],
+                                 [T.xq[:, slot * CH:(slot + 1) * CH]], sem.hq, ms[i]))
+            sent += _count(ms[i])
+        g.remote_dma_fused(trs, local_sem=sem.snt)
     g.wait_ge(sem.pk, npk)
     trs = []
     users = _pack_users(T, topo, core)
     ms = _deal(T, topo, core, [[e] for e in spares] + [users])
-    for i, d in enumerate([s for s in range(len(grp)) if s != slot]):
+    for i in range(len(spares)):
+        d = _served(grp, slot, i)
         trs.append(_transfer(topo, core, [spares[i]], [T.xp[:, d * PK:(d + 1) * PK]], [T.pb[:, :]], sem.hq, ms[i]))
         sent += _count(ms[i])
     trs.append(_transfer(topo, core, users, [T.xp[:, slot * PK:(slot + 1) * PK]],

from concourse.bass import DstId, RemoteDMATransfer
from concourse.mybir import AluOpType

N = 16
CB = 128
W = N * CB
CH = 512
NQ = W // CH
NSLOT = 4
NLD = 2
PK = (NQ - 1) * CB
ORDER = ("opp", "rel", "own", "dir")

SCRATCH = {
    "xs": ("sbuf", [128, W], "bfloat16"),
    "xp": ("sbuf", [128, NSLOT * PK], "bfloat16"),
    "pb": ("sbuf", [128, PK], "bfloat16"),
    "xq": ("sbuf", [128, NSLOT * CH], "bfloat16"),
    "lp": ("sbuf", [128, NSLOT * PK], "bfloat16"),
    "so": ("sbuf", [128, CH], "bfloat16"),
    "sd": ("sbuf", [128, CH], "bfloat16"),
    "sr": ("sbuf", [128, CH], "bfloat16"),
    "sw": ("sbuf", [128, CH], "bfloat16"),
    "lo": ("sbuf", [128, CH], "bfloat16"),
    "ow": ("sbuf", [128, W], "bfloat16"),
    "ls": ("sbuf", [128, W], "bfloat16"),
    "lc": ("sbuf", [128, W], "bfloat16"),
    "ob": ("sbuf", [128, W], "bfloat16"),
}
for _i in range(NQ):
    SCRATCH["ps%d" % _i] = ("psum", [128, CH], "float32")

SEMAPHORES = (["ld%d" % k for k in range(NLD)] + ["pk", "hq", "hp", "co", "snt", "st0", "st1"]
              + ["a%d" % s for s in range(NSLOT)]
              + ["ow%d" % q for q in range(NQ)] + ["sf%d" % q for q in range(NQ)] + ["cd%d" % q for q in range(NQ)]
              + ["tq%d" % q for q in range(NQ)] + ["fin%d" % q for q in range(NQ)]
              + ["pe%d" % k for k in range(NQ)] + ["ev%d" % k for k in range(NQ)])

_MEMO = {}


def _bits(mask):
    return [i for i in range(32) if (mask >> i) & 1]


def _count(mask):
    return len(_bits(mask))


def _one_a_die(topo, cs):
    out, dies = [], set()
    for c in cs:
        if topo.die(c) not in dies:
            dies.add(topo.die(c))
            out.append(c)
    return out


def _crew(T, topo, rc):
    if rc not in _MEMO:
        ncores = (max(topo.host(c) for c in T.cores) + 1) * topo.CORES_PER_HOST
        here = [c for c in range(ncores) if c != rc and topo.host(c) == topo.host(rc) and topo.chip(c) == topo.chip(rc)]
        there = [c for c in range(ncores) if topo.mates(c, rc)]
        spares = [c for c in here if topo.may_write(c, there[0])][:NSLOT - 1]
        load = lambda c: sum(1 for e in spares if topo.die(e) == topo.die(c))
        near = sorted(_one_a_die(topo, [c for c in here if c not in spares]), key=load)
        far = sorted(_one_a_die(topo, [c for c in there if topo.may_write(c, rc)]), key=load)
        _MEMO[rc] = ([near[0], far[0], far[1], near[1]], spares)
    return _MEMO[rc]


def _host_group(T, topo, core):
    return [b for b in range(N) if topo.host(T.cores[b]) == topo.host(core)]


def _roles(T, topo, rc):
    role = {}
    for b in range(N):
        c = T.cores[b]
        if topo.chip(c) != topo.chip(rc):
            continue
        if c == rc:
            role[b] = "own"
        elif not topo.may_write(rc, c):
            role[b] = "opp"
        elif topo.same_plane(rc, c):
            role[b] = "rel"
        else:
            role[b] = "dir"
    return role


def _pieces(T, topo, rc, q):
    role = _roles(T, topo, rc)
    out = []
    for r in ORDER:
        for b in role:
            lo, hi = q * CH, min(q * CH + CH, b * CB)
            if role[b] == r and hi > lo:
                out.append((r, b, lo, hi))
    return out


def _reads(T, topo, rc, q):
    u = 0
    for _, b, lo, hi in _pieces(T, topo, rc, q):
        u = max(u, hi - lo)
        if (b * CB) // CH == q:
            u = max(u, b * CB - q * CH + CB)
    return u


def _packrows(T, topo, rc):
    return [b for b in sorted(_roles(T, topo, rc), reverse=True) if (b * CB) // CH > 0]


def _needs_pack(T, topo, rc, q):
    return any((b * CB) // CH != q for _, b, _, _ in _pieces(T, topo, rc, q))


def _pack_users(T, topo, rc):
    return [_crew(T, topo, rc)[0][q] for q in range(NQ) if _needs_pack(T, topo, rc, q)]


def _pack_classes(T, topo, rc):
    need = {}
    for q in range(NQ):
        if _needs_pack(T, topo, rc, q):
            need[_crew(T, topo, rc)[0][q]] = CB * sum(1 for b in _packrows(T, topo, rc) if (b * CB) // CH > q)
    return [(wd, [c for c in need if need[c] == wd]) for wd in sorted(set(need.values()), reverse=True)]


def _served(grp, slot, i):
    return (slot + 1 + i) % len(grp)


def _per(T, topo, rc, n):
    return _count(topo.mask(rc, _crew(T, topo, rc)[1][0])) // n


def _deal(T, topo, rc, dests):
    per = _per(T, topo, rc, len(dests))
    allowed = []
    for ds in dests:
        m = topo.mask(rc, ds[0])
        for d in ds:
            m &= topo.mask(rc, d)
        allowed.append(m)
    used, out = 0, {}
    for i in sorted(range(len(dests)), key=lambda i: _count(allowed[i])):
        m = sum(1 << e for e in _bits(allowed[i] & ~used)[:per])
        used |= m
        out[i] = m
    return [out[i] for i in range(len(dests))]


def _own_mask(topo, w, rc, off):
    m = topo.mask(w, rc) & ~topo.mask(w, off)
    return m if m else topo.mask(w, rc)


def _transfer(topo, src_core, dsts, srcs, outs, rsem, mask):
    ids = []
    for d in dsts:
        rid, pid = topo.addr(d, src_core)
        ids.append(DstId(rid=rid, pnc=pid))
    return RemoteDMATransfer(dst_ids=ids, dma_engine_mask=mask, remote_sem=rsem, srcs=srcs, dsts=outs,
                             alu_op=1 if len(srcs) > 1 else 0)


def _send(g, T, topo, src_core, dsts, srcs, out, rsem, mask=None):
    m = topo.mask(src_core, dsts[0]) if mask is None else mask
    g.remote_dma_fused([_transfer(topo, src_core, dsts, srcs, [out for _ in dsts], rsem, m)], local_sem=T.sem.snt)
    return _count(m)


def _spare_program(g, core, T, topo, rank, i):
    rc = T.cores[rank]
    grp = _host_group(T, topo, rc)
    slot = grp.index(rank)
    peer = T.cores[grp[_served(grp, slot, i)]]
    g.wait_ge(T.sem.hq, _per(T, topo, rc, NSLOT))
    n = 0
    for wd, users in _pack_classes(T, topo, peer):
        n += _send(g, T, topo, core, users, [T.pb[:, 0:wd]], T.lp[:, slot * PK:slot * PK + wd], T.sem["a%d" % slot])
    g.wait_ge(T.sem.snt, n)


def _worker_program(g, core, T, topo, rank, q):
    sem = T.sem
    rc = T.cores[rank]
    grp = _host_group(T, topo, rc)
    slot = grp.index(rank)
    others = [(slot - d) % len(grp) for d in range(1, len(grp))]
    role = _roles(T, topo, rc)
    cable = [T.cores[b] for b in role if role[b] == "dir"][0]
    neigh = [T.cores[b] for b in role if role[b] == "rel"][0]
    twin = _crew(T, topo, neigh)[0][q]
    pcs = _pieces(T, topo, rc, q)
    pack = _needs_pack(T, topo, rc, q)
    prow = _packrows(T, topo, rc)
    nh = _per(T, topo, rc, NQ // NLD)
    nhp = _per(T, topo, rc, NSLOT)
    bank = [T["ps%d" % i] for i in range(len(pcs))]

    sent = 0
    g.wait_ge(sem.hq, nh)
    for d in range(1, len(grp)):
        peer = T.cores[grp[(slot + d) % len(grp)]]
        u = _reads(T, topo, peer, q)
        if u:
            part = T.xq[:, slot * CH:slot * CH + u]
            sent += _send(g, T, topo, core, [_crew(T, topo, peer)[0][q]], [part], part, sem["a%d" % slot])

    te = g.tensor

    def mm(i, s, start, stop):
        _, b, lo, hi = pcs[i]
        if (b * CB) // CH == q:
            o = s * CH + b * CB - q * CH
            lhs = T.xq[:, o:o + CB]
        else:
            o = s * PK + prow.index(b) * CB
            lhs = T.lp[:, o:o + CB]
        return te.matmul(bank[i][:, 0:hi - lo], lhs, T.xq[:, s * CH:s * CH + hi - lo], start=start, stop=stop)

    def landed(s):
        src = T.cores[grp[s]]
        n = _count(topo.mask(_crew(T, topo, src)[0][q], core))
        if pack:
            n += _count(topo.mask(_crew(T, topo, src)[1][0], core))
        te.wait_ge(sem["a%d" % s], n)

    if pcs:
        te.wait_ge(sem.hq, nh)
        if pack:
            te.wait_ge(sem.hp, nhp)
        for i in range(len(pcs)):
            mm(i, slot, True, False)
        landed(others[0])
        for i in range(len(pcs)):
            mm(i, others[0], False, False)
        late = others[1:]
        for i in range(len(pcs)):
            for s in late:
                if i == 0:
                    landed(s)
                ins = mm(i, s, False, s == late[-1])
            ins.then_inc(sem["pe%d" % i], 1)

    stage = {"opp": T.so, "dir": T.sd, "rel": T.sr, "own": T.sw}
    for i, (r, b, lo, hi) in enumerate(pcs):
        g.vector.wait_ge(sem["pe%d" % i], 1)
        g.vector.tensor_copy(stage[r][:, 0:hi - lo], bank[i][:, 0:hi - lo]).then_inc(sem["ev%d" % i], 1)

    for i, (r, b, lo, hi) in enumerate(pcs):
        w = hi - lo
        g.wait_ge(sem["ev%d" % i], 1)
        if r == "opp":
            sent += _send(g, T, topo, core, [twin], [T.so[:, 0:w]], T.lo[:, 0:w], sem.co)
        elif r == "dir":
            g.wait_ge(sem.co, _count(topo.mask(twin, core)))
            sent += _send(g, T, topo, core, [cable], [T.sd[:, 0:w], T.lo[:, 0:w]], T.lc[:, lo:hi], sem["cd%d" % q])
        elif r == "rel":
            sent += _send(g, T, topo, core, [neigh], [T.sr[:, 0:w]], T.ls[:, lo:hi], sem["sf%d" % q])
        else:
            sent += _send(g, T, topo, core, [rc], [T.sw[:, 0:w]], T.ow[:, lo:hi], sem["ow%d" % q],
                          mask=_own_mask(topo, core, rc, neigh))
    g.wait_ge(sem.snt, sent)


def rank_program(g, core, T, topo):
    rank = T.rank_of(core)
    if rank is None:
        for b in range(N):
            rc = T.cores[b]
            if topo.host(rc) == topo.host(core):
                workers, spares = _crew(T, topo, rc)
                if core in workers:
                    _worker_program(g, core, T, topo, b, workers.index(core))
                elif core in spares:
                    _spare_program(g, core, T, topo, b, spares.index(core))
        return
    sem = T.sem
    grp = _host_group(T, topo, core)
    slot = grp.index(rank)
    workers, spares = _crew(T, topo, core)
    role = _roles(T, topo, core)
    cable = [T.cores[b] for b in role if role[b] == "dir"][0]
    neigh = [T.cores[b] for b in role if role[b] == "rel"][0]
    ve = g.vector

    LW = W // NLD
    lq = [g.sync, g.scalar]
    for k in range(NLD):
        lq[k % 2].dma_start(T.xs[:, k * LW:(k + 1) * LW], T.x[:, k * LW:(k + 1) * LW]).then_inc(sem["ld%d" % k], 16)

    for k in range(NLD):
        ve.wait_ge(sem["ld%d" % k], 16)
    npk = 0
    for d in [s for s in range(len(grp)) if s != slot] + [slot]:
        for j, b in enumerate(_packrows(T, topo, T.cores[grp[d]])):
            ve.tensor_copy(T.xp[:, d * PK + j * CB:d * PK + (j + 1) * CB], T.xs[:, b * CB:(b + 1) * CB]).then_inc(sem.pk, 1)
            npk += 1

    sent = 0
    for k in range(NLD):
        qs = list(range(k * NQ // NLD, (k + 1) * NQ // NLD))
        g.wait_ge(sem["ld%d" % k], 16)
        ms = _deal(T, topo, core, [[workers[q]] for q in qs])
        trs = []
        for i, q in enumerate(qs):
            trs.append(_transfer(topo, core, [workers[q]], [T.xs[:, q * CH:(q + 1) * CH]],
                                 [T.xq[:, slot * CH:(slot + 1) * CH]], sem.hq, ms[i]))
            sent += _count(ms[i])
        g.remote_dma_fused(trs, local_sem=sem.snt)
    g.wait_ge(sem.pk, npk)
    trs = []
    users = _pack_users(T, topo, core)
    ms = _deal(T, topo, core, [[e] for e in spares] + [users])
    for i in range(len(spares)):
        d = _served(grp, slot, i)
        trs.append(_transfer(topo, core, [spares[i]], [T.xp[:, d * PK:(d + 1) * PK]], [T.pb[:, :]], sem.hq, ms[i]))
        sent += _count(ms[i])
    trs.append(_transfer(topo, core, users, [T.xp[:, slot * PK:(slot + 1) * PK]],
                         [T.lp[:, slot * PK:(slot + 1) * PK] for _ in users], sem.hp, ms[-1]))
    sent += _count(ms[-1])
    g.remote_dma_fused(trs, local_sem=sem.snt)
    g.wait_ge(sem.snt, sent)

    mine = [(q, q * CH, min(q * CH + CH, rank * CB)) for q in reversed(range(NQ)) if rank * CB > q * CH]

    def first(q, lo, hi):
        ve.wait_ge(sem["ow%d" % q], _count(_own_mask(topo, workers[q], core, neigh)))
        ve.wait_ge(sem["sf%d" % q], _count(topo.mask(_crew(T, topo, neigh)[0][q], core)))
        ve.tensor_tensor(T["ps%d" % q][:, 0:hi - lo], T.ow[:, lo:hi], T.ls[:, lo:hi], AluOpType.add).then_inc(sem["tq%d" % q], 1)

    def last(q, lo, hi):
        ve.wait_ge(sem["tq%d" % q], 1)
        ve.wait_ge(sem["cd%d" % q], _count(topo.mask(_crew(T, topo, cable)[0][q], core)))
        ve.tensor_tensor(T.ob[:, lo:hi], T["ps%d" % q][:, 0:hi - lo], T.lc[:, lo:hi], AluOpType.add).then_inc(sem["fin%d" % q], 1)

    for p in mine:
        first(*p)
    for p in mine:
        last(*p)

    queues = [g.sync, g.scalar]
    nst = [0, 0]
    for k, (q, lo, hi) in enumerate(mine):
        e = k % 2
        queues[e].wait_ge(sem["fin%d" % q], 1)
        queues[e].dma_start(T.y[:, lo:hi], T.ob[:, lo:hi]).then_inc(sem["st%d" % e], 16)
        nst[e] += 16
    for e in range(2):
        if nst[e]:
            queues[e].wait_ge(sem["st%d" % e], nst[e])
